import numpy as np
import ml_dtypes


def mxq(x, axis, fmt="e4m3"):
    dtype, down = {"e4m3": (ml_dtypes.float8_e4m3fn, 7), "e5m2": (ml_dtypes.float8_e5m2, 14)}[fmt]
    v = np.moveaxis(np.asarray(x, np.float32).astype(ml_dtypes.bfloat16).astype(np.float64), axis, -1)
    blocks = v.reshape(v.shape[:-1] + (-1, 32))
    amax = np.abs(blocks).max(-1, keepdims=True)
    byte = np.maximum(np.where(amax > 0, np.frexp(amax)[1] - 1 + 127, 0) - down, 1)
    scale = np.exp2(byte - 127.0)
    codes = (blocks / scale).astype(np.float32).astype(dtype).astype(np.float64)
    return np.moveaxis((codes * scale).reshape(v.shape), -1, axis)


WIDE = False


def mx_kscale(k, group=512):
    if not WIDE:
        return np.ones(k)
    levels = np.array([10, -10, 5, -5, 0])
    if group != 512:
        return np.exp2(np.random.permutation(np.resize(levels, k // group))).repeat(group)
    if k % 512:
        return np.exp2(np.random.permutation(np.resize(levels, k // 32))).repeat(32)
    a = np.empty((k // 512, 16))
    for p in range(k // 512):
        a[p, :8] = np.random.permutation(np.resize(levels, 8))
        for g in range(8):
            far = levels[np.abs(levels - a[p, g]) >= 10]
            a[p, g + 8] = far[np.random.randint(len(far))]
    return np.exp2(a.ravel()).repeat(32)


def f64(x):
    return np.asarray(x).astype(np.float64)


def striped(idx):
    return np.tile(np.asarray(idx).reshape(-1, 16).T, (8, 1)).astype(np.uint16)


def unstriped(offs):
    return offs[:16].T.reshape(-1).astype(np.int64)


H, KV, D, NQ, N = 2, 2, 256, 512, 1024
CAP = 2.0


def setup_inputs():
    n = np.random.standard_normal
    s = mx_kscale(D, 0)[:, None]
    u = mx_kscale(N)
    t = np.random.uniform(0.5, 2.0, N) * u
    v = n((KV, N, 128))
    return {
        "qT": (n((H, D, NQ)) * s * (0.70 / np.sqrt(D))).astype(np.float32),
        "kT": (n((KV, D, N)) / s).astype(np.float32),
        "t": t.reshape(N, 1).astype(np.float32),
        "v": (v / t[:, None]).astype(np.float32),
        "gn": np.tile(np.random.uniform(0.5, 2.0, 128), (128, 1)).astype(np.float32),
    }


def reference(qT, kT, t, v, gn):
    a = mxq(f64(kT), 1, "e4m3").transpose(0, 2, 1) @ mxq(f64(qT), 1, "e4m3")
    a = CAP * np.tanh(a / CAP)
    p = np.maximum(a, 0.0)
    w = p * f64(t)
    y = mxq(w, 1, "e4m3").transpose(0, 2, 1) @ mxq(f64(v), 1, "e4m3")
    y = y / 16.0
    y = y / np.sqrt(np.mean(np.square(y), -1, keepdims=True) + 1e-5) * f64(gn)[:1]
    return y

@@ -1,0 +1,261 @@
+from contextlib import ExitStack
+
+import concourse.mybir as mybir
+
+H, D, NQ, N, E = 2, 256, 512, 1024, 128
+FLOPS = 2 * H * N * NQ * (D + E)
+
+F32 = mybir.dt.float32
+BF16 = mybir.dt.bfloat16
+U32 = mybir.dt.uint32
+U8 = mybir.dt.uint8
+FP8X4 = mybir.dt.float8_e4m3fn_x4
+ACT = mybir.ActivationFunctionType
+ALU = mybir.AluOpType
+
+P = 128
+PACK = 4
+ROWS = D // PACK
+PASS = P * PACK
+PASSES = N // PASS
+QT = 128
+QTILES = NQ // QT
+UNITS = PASSES * QTILES * H
+HALF = PASS // 2
+
+
+def tile_rows_a_relu_cap_onorm_kernel(tc, qT, kT, t, v, gn, out):
+    nc = tc.nc
+    with ExitStack() as ctx:
+        sb = ctx.enter_context(tc.tile_pool(name="sb", bufs=1))
+        ps = ctx.enter_context(tc.psum_pool(name="ps", bufs=1))
+        ctx.enter_context(tc.manual_schedule())
+
+        def tile(name, shape, dtype):
+            return sb.tile(shape, dtype, name=name, align_bytes=64)
+
+        q_hbm = qT.rearrange("h (p j) q -> (h p) j q", j=PACK)
+        k_hbm = kT.rearrange("h (p j) n -> (h p) j n", j=PACK)
+        v_hbm = v.rearrange("h (g p j) e -> g p h (j e)", g=PASSES, j=PACK)
+        t_hbm = t.rearrange("(g p j) o -> p g (j o)", g=PASSES, j=PACK)
+
+        q_raw0 = tile("q_raw0", [P, PACK, QT], F32)
+        q_raw1 = tile("q_raw1", [P, PACK, QT], F32)
+        q_raw23 = tile("q_raw23", [P, PACK, 2 * QT], F32)
+        q_raw = [q_raw0[:], q_raw1[:], q_raw23[:, :, :QT], q_raw23[:, :, QT:]]
+        k_raw = [[tile(f"k_raw{g}{c}", [P, PACK, HALF], F32) for c in range(2)] for g in range(PASSES)]
+        v_raw = [tile(f"v_raw{g}", [P, H, PACK * E], F32) for g in range(PASSES)]
+        t_raw = tile("t_raw", [P, PASSES, PACK], F32)
+        t2 = tile("t2", [P, PASSES, PACK], F32)
+        gain = tile("gain", [P, E], F32)
+
+        q_bf = [tile(f"q_bf{i}", [P, QT * PACK], BF16) for i in range(QTILES)]
+        q_codes = [tile(f"q_codes{i}", [P, QT], U32) for i in range(QTILES)]
+        q_scales = [tile(f"q_scales{i}", [P, QT], U8) for i in range(QTILES)]
+        k_bf = [tile(f"k_bf{g}", [P, PACK, P, PACK], BF16) for g in range(PASSES)]
+        k_codes = [tile(f"k_codes{g}", [P, PASS], U32) for g in range(PASSES)]
+        k_scales = [tile(f"k_scales{g}", [P, PASS], U8) for g in range(PASSES)]
+        v_bf = [tile(f"v_bf{g}", [P, H, E * PACK], BF16) for g in range(PASSES)]
+        v_codes = [tile(f"v_codes{g}", [P, H * E], U32) for g in range(PASSES)]
+        v_scales = [tile(f"v_scales{g}", [P, H * E], U8) for g in range(PASSES)]
+        capped = [tile(f"capped{u}", [P, QT, PACK], F32) for u in range(UNITS)]
+        w_bf = [tile(f"w_bf{u}", [P, QT, PACK], BF16) for u in range(UNITS)]
+        w_codes = [tile(f"w_codes{u}", [P, QT], U32) for u in range(UNITS)]
+        w_scales = [tile(f"w_scales{u}", [P, QT], U8) for u in range(UNITS)]
+        squares = tile("squares", [P, E], BF16)
+        sumsq = tile("sumsq", [P, QTILES * H], F32)
+        rstd = tile("rstd", [P, QTILES * H], F32)
+        result = [tile(f"result{i}", [P, H, E], F32) for i in range(QTILES)]
+        warm = tile("warm", [P, 1], F32)
+        warm_out = tile("warm_out", [P, 1], F32)
+
+        s_bank = [[ps.tile([P, PACK * QT], F32, name=f"s_bank{h}{b}") for b in range(2)] for h in range(H)]
+        y_bank = [ps.tile([P, 4 * E], F32, name=f"y_bank{b}") for b in range(4)]
+        y_place = [(0, 0), (0, 1), (0, 2), (0, 3), (1, 0), (1, 1), (2, 0), (3, 0)]
+
+        def y_ap(o):
+            b, c = y_place[o]
+            return y_bank[b][:, c * E:(c + 1) * E]
+
+        def copy(eng, dst, src):
+            if eng is nc.scalar:
+                nc.scalar.copy(out=dst, in_=src)
+            else:
+                nc.vector.tensor_copy(out=dst, in_=src)
+
+        def interleave(eng, dst, src):
+            copy(eng, dst.rearrange("p (c i j) -> p c j i", i=4, j=PACK), src.rearrange("p j (c i) -> p c j i", i=4))
+
+        def cast_q(eng, i):
+            interleave(eng, q_bf[i][:], q_raw[i])
+
+        def cast_v(eng, g, h):
+            interleave(eng, v_bf[g][:, h, :], v_raw[g][:, h, :].rearrange("p (j e) -> p j e", j=PACK))
+
+        def cast_k(eng, g, c, s0, s1):
+            dst = k_bf[g][:, :, 64 * c + s0:64 * c + s1, :].rearrange("p r s j -> p s j r")
+            src = k_raw[g][c][:, :, PACK * s0:PACK * s1].rearrange("p j (s r) -> p s j r", r=PACK)
+            copy(eng, dst, src)
+
+        def quant(codes, scales, src):
+            nc.vector.quantize_mx(out=codes.bitcast(FP8X4), scales=scales, in_=src)
+
+        def quant_q(i):
+            quant(q_codes[i][:], q_scales[i][:], q_bf[i][:])
+
+        def quant_k(g, col0, cols):
+            flat = k_bf[g][:].rearrange("p r s j -> p (r s j)")
+            quant(k_codes[g][:, col0:col0 + cols], k_scales[g][:, col0:col0 + cols], flat[:, PACK * col0:PACK * (col0 + cols)])
+
+        def quant_v(g):
+            quant(v_codes[g][:], v_scales[g][:], v_bf[g][:].rearrange("p h x -> p (h x)"))
+
+        def quant_w(u):
+            quant(w_codes[u][:], w_scales[u][:], w_bf[u][:].rearrange("p q r -> p (q r)"))
+
+        def unit(u):
+            return u // (QTILES * H), (u // H) % QTILES, u % H
+
+        def score_r(u, r):
+            g, i, h = unit(u)
+            rows = slice(ROWS * h, ROWS * (h + 1))
+            cols = slice(P * r, P * (r + 1))
+            nc.tensor.matmul_mx(
+                out=s_bank[h][(u // H) % 2][:, QT * r:QT * (r + 1)],
+                lhsT=k_codes[g][rows, cols].bitcast(FP8X4),
+                lhsT_scale=k_scales[g][rows, cols],
+                rhs=q_codes[i][rows, :].bitcast(FP8X4),
+                rhs_scale=q_scales[i][rows, :],
+                start=True,
+                stop=True,
+            )
+
+        def score_pair(u):
+            for r in range(PACK):
+                score_r(u, r)
+                score_r(u + 1, r)
+
+        def cap(u):
+            g, i, h = unit(u)
+            src = s_bank[h][(u // H) % 2][:].rearrange("p (r q) -> p q r", r=PACK)
+            nc.scalar.activation(out=capped[u][:], in_=src, func=ACT.Tanh, scale=0.5)
+
+        def weigh(u):
+            g, i, h = unit(u)
+            nc.vector.scalar_tensor_tensor(
+                out=w_bf[u][:],
+                in0=capped[u][:],
+                scalar=0.0,
+                in1=t2[:, g:g + 1, :].broadcast_to([P, QT, PACK]),
+                op0=ALU.max,
+                op1=ALU.mult,
+            )
+
+        def mix(o):
+            h = o % H
+            cols = slice(E * h, E * (h + 1))
+            for g in range(PASSES):
+                u = g * QTILES * H + o
+                nc.tensor.matmul_mx(
+                    out=y_ap(o),
+                    lhsT=w_codes[u][:].bitcast(FP8X4),
+                    lhsT_scale=w_scales[u][:],
+                    rhs=v_codes[g][:, cols].bitcast(FP8X4),
+                    rhs_scale=v_scales[g][:, cols],
+                    start=(g == 0),
+                    stop=(g == PASSES - 1),
+                )
+
+        def square(o):
+            nc.scalar.activation(out=squares[:], in_=y_ap(o), func=ACT.Square, scale=1.0 / 16.0, accum_out=sumsq[:, o:o + 1])
+
+        def norm(o0, o1):
+            nc.scalar.activation(out=rstd[:, o0:o1], in_=sumsq[:, o0:o1], func=ACT.Abs_reciprocal_sqrt, scale=256.0 / E, bias=256.0 * 1e-5)
+
+        def finish(o):
+            nc.vector.scalar_tensor_tensor(
+                out=result[o // H][:, o % H, :], in0=y_ap(o), scalar=rstd[:, o:o + 1], in1=gain[:], op0=ALU.mult, op1=ALU.mult
+            )
+
+        def store(i, h0, h1):
+            nc.sync.dma_start(out=out[h0:h1, QT * i:QT * (i + 1), :].rearrange("h q e -> q h e"), in_=result[i][:, h0:h1, :])
+
+        nc.gpsimd.memset(warm[:], 0.0)
+        nc.scalar.activation(out=warm_out[:], in_=warm[:], func=ACT.Tanh)
+        nc.sync.dma_start(out=q_raw0[:], in_=q_hbm[:, :, 0:QT])
+        nc.scalar.dma_start(out=t_raw[:], in_=t_hbm)
+        for c in range(2):
+            nc.sync.dma_start(out=k_raw[0][c][:], in_=k_hbm[:, :, HALF * c:HALF * (c + 1)])
+        nc.sync.dma_start(out=q_raw1[:], in_=q_hbm[:, :, QT:2 * QT])
+        nc.sync.dma_start(out=q_raw23[:], in_=q_hbm[:, :, 2 * QT:])
+        for c in range(2):
+            nc.sync.dma_start(out=k_raw[1][c][:], in_=k_hbm[:, :, PASS + HALF * c:PASS + HALF * (c + 1)])
+        for g in range(PASSES):
+            nc.sync.dma_start(out=v_raw[g][:], in_=v_hbm[g])
+        nc.sync.dma_start(out=gain[:], in_=gn)
+
+        S, V = nc.scalar, nc.vector
+        cast_q(V, 0)
+        nc.vector.tensor_scalar(out=t2[:], in0=t_raw[:], scalar1=2.0, scalar2=None, op0=ALU.mult)
+        quant_q(0)
+        for c in range(2):
+            cast_k(V, 0, c, 0, 44)
+            cast_k(S, 0, c, 44, 64)
+            for r in range(PACK):
+                quant_k(0, P * r + 64 * c, 64)
+        score_pair(0)
+        cast_q(V, 1)
+        quant_q(1)
+        score_pair(2)
+
+        s_extra = {
+            1: [lambda: cast_q(S, 3)],
+            2: [lambda: cast_k(S, 1, 0, 0, 32)],
+            3: [lambda: cast_k(S, 1, 0, 32, 64)],
+            7: [lambda: cast_v(S, 0, 0), lambda: cast_v(S, 0, 1)],
+            8: [lambda: cast_v(S, 1, 0)],
+            9: [lambda: cast_v(S, 1, 1)],
+            12: [lambda: square(0)],
+            13: [lambda: square(1), lambda: square(2)],
+            14: [lambda: square(3)],
+        }
+        v_extra = {
+            0: [lambda: cast_q(V, 2)],
+            1: [lambda: quant_q(2), lambda: score_pair(4)],
+            2: [lambda: quant_q(3)],
+            3: [lambda: cast_k(V, 1, 1, 0, 32), lambda: score_pair(6)],
+            4: [lambda: cast_k(V, 1, 1, 32, 64)],
+            5: [lambda: quant_k(1, 0, PASS), lambda: score_pair(8)],
+            7: [lambda: score_pair(10)],
+            8: [lambda: quant_v(0)],
+            9: [lambda: quant_v(1), lambda: score_pair(12)],
+            11: [lambda: score_pair(14), lambda: mix(0), lambda: mix(1), lambda: mix(2)],
+            12: [lambda: mix(3)],
+            13: [lambda: mix(4)],
+            14: [lambda: mix(5)],
+        }
+        for u in range(UNITS):
+            cap(u)
+            for job in s_extra.get(u, []):
+                job()
+            weigh(u)
+            if u > 0:
+                quant_w(u - 1)
+            for job in v_extra.get(u, []):
+                job()
+        mix(6)
+        quant_w(UNITS - 1)
+        mix(7)
+        square(4)
+        norm(0, 5)
+        square(5)
+        square(6)
+        norm(5, 7)
+        square(7)
+        norm(7, 8)
+        for o in range(QTILES * H):
+            finish(o)
+            if o in (1, 3, 5):
+                store(o // H, 0, H)
+            elif o >= 6:
+                store(o // H, o % H, o % H + 1)

@@ -42,27 +42,27 @@ def tile_rows_a_relu_cap_onorm_kernel(tc, qT, kT, t, v, gn, out):
         q_raw0 = tile("q_raw0", [P, PACK, QT], F32)
         q_raw1 = tile("q_raw1", [P, PACK, QT], F32)
         q_raw23 = tile("q_raw23", [P, PACK, 2 * QT], F32)
-        q_raw = [q_raw0[:], q_raw1[:], q_raw23[:, :, :QT], q_raw23[:, :, QT:]]
+        q_raw = {0: q_raw0, 1: q_raw1, 2: q_raw23, 3: q_raw23}
         k_raw = [[tile(f"k_raw{g}{c}", [P, PACK, HALF], F32) for c in range(2)] for g in range(PASSES)]
         v_raw = [tile(f"v_raw{g}", [P, H, PACK * E], F32) for g in range(PASSES)]
         t_raw = tile("t_raw", [P, PASSES, PACK], F32)
         t2 = tile("t2", [P, PASSES, PACK], F32)
         gain = tile("gain", [P, E], F32)
 
-        q_bf = [tile(f"q_bf{i}", [P, QT * PACK], BF16) for i in range(QTILES)]
-        q_codes = [tile(f"q_codes{i}", [P, QT], U32) for i in range(QTILES)]
-        q_scales = [tile(f"q_scales{i}", [P, QT], U8) for i in range(QTILES)]
+        q_bf = tile("q_bf", [P, NQ * PACK], BF16)
+        q_codes = tile("q_codes", [P, NQ], U32)
+        q_scales = tile("q_scales", [P, NQ], U8)
         k_bf = [tile(f"k_bf{g}", [P, PACK, P, PACK], BF16) for g in range(PASSES)]
         k_codes = [tile(f"k_codes{g}", [P, PASS], U32) for g in range(PASSES)]
         k_scales = [tile(f"k_scales{g}", [P, PASS], U8) for g in range(PASSES)]
-        v_bf = [tile(f"v_bf{g}", [P, H, E * PACK], BF16) for g in range(PASSES)]
-        v_codes = [tile(f"v_codes{g}", [P, H * E], U32) for g in range(PASSES)]
-        v_scales = [tile(f"v_scales{g}", [P, H * E], U8) for g in range(PASSES)]
-        capped = [tile(f"capped{u}", [P, QT, PACK], F32) for u in range(UNITS)]
-        w_bf = [tile(f"w_bf{u}", [P, QT, PACK], BF16) for u in range(UNITS)]
-        w_codes = [tile(f"w_codes{u}", [P, QT], U32) for u in range(UNITS)]
-        w_scales = [tile(f"w_scales{u}", [P, QT], U8) for u in range(UNITS)]
-        squares = tile("squares", [P, E], BF16)
+        v_bf = tile("v_bf", [P, PASSES * H, E * PACK], BF16)
+        v_codes = tile("v_codes", [P, PASSES * H * E], U32)
+        v_scales = tile("v_scales", [P, PASSES * H * E], U8)
+        capped = tile("capped", [P, UNITS * QT, PACK], F32)
+        w_bf = tile("w_bf", [P, UNITS * QT, PACK], BF16)
+        w_codes = tile("w_codes", [P, UNITS * QT], U32)
+        w_scales = tile("w_scales", [P, UNITS * QT], U8)
+        squares = tile("squares", [P, QTILES * H, E], BF16)
         sumsq = tile("sumsq", [P, QTILES * H], F32)
         rstd = tile("rstd", [P, QTILES * H], F32)
         result = [tile(f"result{i}", [P, H, E], F32) for i in range(QTILES)]
@@ -71,7 +71,7 @@ def tile_rows_a_relu_cap_onorm_kernel(tc, qT, kT, t, v, gn, out):
 
         s_bank = [[ps.tile([P, PACK * QT], F32, name=f"s_bank{h}{b}") for b in range(2)] for h in range(H)]
         y_bank = [ps.tile([P, 4 * E], F32, name=f"y_bank{b}") for b in range(4)]
-        y_place = [(0, 0), (0, 1), (0, 2), (0, 3), (1, 0), (1, 1), (2, 0), (3, 0)]
+        y_place = [(0, 0), (0, 1), (1, 0), (1, 1), (2, 0), (2, 1), (3, 0), (3, 1)]
 
         def y_ap(o):
             b, c = y_place[o]
@@ -86,11 +86,12 @@ def tile_rows_a_relu_cap_onorm_kernel(tc, qT, kT, t, v, gn, out):
         def interleave(eng, dst, src):
             copy(eng, dst.rearrange("p (c i j) -> p c j i", i=4, j=PACK), src.rearrange("p j (c i) -> p c j i", i=4))
 
-        def cast_q(eng, i):
-            interleave(eng, q_bf[i][:], q_raw[i])
+        def cast_q(eng, q0, q1):
+            first = min(q0 // QT, 2) * QT
+            interleave(eng, q_bf[:, PACK * q0:PACK * q1], q_raw[q0 // QT][:, :, q0 - first:q1 - first])
 
         def cast_v(eng, g, h):
-            interleave(eng, v_bf[g][:, h, :], v_raw[g][:, h, :].rearrange("p (j e) -> p j e", j=PACK))
+            interleave(eng, v_bf[:, H * g + h, :], v_raw[g][:, h, :].rearrange("p (j e) -> p j e", j=PACK))
 
         def cast_k(eng, g, c, s0, s1):
             dst = k_bf[g][:, :, 64 * c + s0:64 * c + s1, :].rearrange("p r s j -> p s j r")
@@ -100,18 +101,19 @@ def tile_rows_a_relu_cap_onorm_kernel(tc, qT, kT, t, v, gn, out):
         def quant(codes, scales, src):
             nc.vector.quantize_mx(out=codes.bitcast(FP8X4), scales=scales, in_=src)
 
-        def quant_q(i):
-            quant(q_codes[i][:], q_scales[i][:], q_bf[i][:])
+        def quant_q(q0, q1):
+            quant(q_codes[:, q0:q1], q_scales[:, q0:q1], q_bf[:, PACK * q0:PACK * q1])
 
         def quant_k(g, col0, cols):
             flat = k_bf[g][:].rearrange("p r s j -> p (r s j)")
             quant(k_codes[g][:, col0:col0 + cols], k_scales[g][:, col0:col0 + cols], flat[:, PACK * col0:PACK * (col0 + cols)])
 
-        def quant_v(g):
-            quant(v_codes[g][:], v_scales[g][:], v_bf[g][:].rearrange("p h x -> p (h x)"))
+        def quant_v(a, b):
+            quant(v_codes[:, E * a:E * b], v_scales[:, E * a:E * b], v_bf[:, a:b, :].rearrange("p h x -> p (h x)"))
 
-        def quant_w(u):
-            quant(w_codes[u][:], w_scales[u][:], w_bf[u][:].rearrange("p q r -> p (q r)"))
+        def quant_w(a, b):
+            cols = slice(QT * a, QT * b)
+            quant(w_codes[:, cols], w_scales[:, cols], w_bf[:, cols, :].rearrange("p q r -> p (q r)"))
 
         def unit(u):
             return u // (QTILES * H), (u // H) % QTILES, u % H
@@ -124,11 +126,15 @@ def tile_rows_a_relu_cap_onorm_kernel(tc, qT, kT, t, v, gn, out):
                 out=s_bank[h][(u // H) % 2][:, QT * r:QT * (r + 1)],
                 lhsT=k_codes[g][rows, cols].bitcast(FP8X4),
                 lhsT_scale=k_scales[g][rows, cols],
-                rhs=q_codes[i][rows, :].bitcast(FP8X4),
-                rhs_scale=q_scales[i][rows, :],
+                rhs=q_codes[rows, QT * i:QT * (i + 1)].bitcast(FP8X4),
+                rhs_scale=q_scales[rows, QT * i:QT * (i + 1)],
                 start=True,
                 stop=True,
             )
+
+        def score(u):
+            for r in range(PACK):
+                score_r(u, r)
 
         def score_pair(u):
             for r in range(PACK):
@@ -138,36 +144,37 @@ def tile_rows_a_relu_cap_onorm_kernel(tc, qT, kT, t, v, gn, out):
         def cap(u):
             g, i, h = unit(u)
             src = s_bank[h][(u // H) % 2][:].rearrange("p (r q) -> p q r", r=PACK)
-            nc.scalar.activation(out=capped[u][:], in_=src, func=ACT.Tanh, scale=0.5)
+            nc.scalar.activation(out=capped[:, QT * u:QT * (u + 1), :], in_=src, func=ACT.Tanh, scale=0.5)
 
-        def weigh(u):
-            g, i, h = unit(u)
+        def weigh(a, b):
+            g = a // (QTILES * H)
+            cols = slice(QT * a, QT * b)
             nc.vector.scalar_tensor_tensor(
-                out=w_bf[u][:],
-                in0=capped[u][:],
+                out=w_bf[:, cols, :],
+                in0=capped[:, cols, :],
                 scalar=0.0,
-                in1=t2[:, g:g + 1, :].broadcast_to([P, QT, PACK]),
+                in1=t2[:, g:g + 1, :].broadcast_to([P, QT * (b - a), PACK]),
                 op0=ALU.max,
                 op1=ALU.mult,
             )
 
         def mix(o):
             h = o % H
-            cols = slice(E * h, E * (h + 1))
             for g in range(PASSES):
                 u = g * QTILES * H + o
+                cols = slice(E * (H * g + h), E * (H * g + h + 1))
                 nc.tensor.matmul_mx(
                     out=y_ap(o),
-                    lhsT=w_codes[u][:].bitcast(FP8X4),
-                    lhsT_scale=w_scales[u][:],
-                    rhs=v_codes[g][:, cols].bitcast(FP8X4),
-                    rhs_scale=v_scales[g][:, cols],
+                    lhsT=w_codes[:, QT * u:QT * (u + 1)].bitcast(FP8X4),
+                    lhsT_scale=w_scales[:, QT * u:QT * (u + 1)],
+                    rhs=v_codes[:, cols].bitcast(FP8X4),
+                    rhs_scale=v_scales[:, cols],
                     start=(g == 0),
                     stop=(g == PASSES - 1),
                 )
 
         def square(o):
-            nc.scalar.activation(out=squares[:], in_=y_ap(o), func=ACT.Square, scale=1.0 / 16.0, accum_out=sumsq[:, o:o + 1])
+            nc.scalar.activation(out=squares[:, o, :], in_=y_ap(o), func=ACT.Square, scale=1.0 / 16.0, accum_out=sumsq[:, o:o + 1])
 
         def norm(o0, o1):
             nc.scalar.activation(out=rstd[:, o0:o1], in_=sumsq[:, o0:o1], func=ACT.Abs_reciprocal_sqrt, scale=256.0 / E, bias=256.0 * 1e-5)
@@ -180,82 +187,125 @@ def tile_rows_a_relu_cap_onorm_kernel(tc, qT, kT, t, v, gn, out):
         def store(i, h0, h1):
             nc.sync.dma_start(out=out[h0:h1, QT * i:QT * (i + 1), :].rearrange("h q e -> q h e"), in_=result[i][:, h0:h1, :])
 
-        nc.gpsimd.memset(warm[:], 0.0)
-        nc.scalar.activation(out=warm_out[:], in_=warm[:], func=ACT.Tanh)
-        nc.sync.dma_start(out=q_raw0[:], in_=q_hbm[:, :, 0:QT])
-        nc.scalar.dma_start(out=t_raw[:], in_=t_hbm)
-        for c in range(2):
-            nc.sync.dma_start(out=k_raw[0][c][:], in_=k_hbm[:, :, HALF * c:HALF * (c + 1)])
-        nc.sync.dma_start(out=q_raw1[:], in_=q_hbm[:, :, QT:2 * QT])
-        nc.sync.dma_start(out=q_raw23[:], in_=q_hbm[:, :, 2 * QT:])
-        for c in range(2):
-            nc.sync.dma_start(out=k_raw[1][c][:], in_=k_hbm[:, :, PASS + HALF * c:PASS + HALF * (c + 1)])
-        for g in range(PASSES):
-            nc.sync.dma_start(out=v_raw[g][:], in_=v_hbm[g])
-        nc.sync.dma_start(out=gain[:], in_=gn)
+        def load(eng, dst, src):
+            eng.dma_start(out=dst, in_=src)
 
         S, V = nc.scalar, nc.vector
-        cast_q(V, 0)
-        nc.vector.tensor_scalar(out=t2[:], in0=t_raw[:], scalar1=2.0, scalar2=None, op0=ALU.mult)
-        quant_q(0)
-        for c in range(2):
-            cast_k(V, 0, c, 0, 44)
-            cast_k(S, 0, c, 44, 64)
-            for r in range(PACK):
-                quant_k(0, P * r + 64 * c, 64)
-        score_pair(0)
-        cast_q(V, 1)
-        quant_q(1)
-        score_pair(2)
+        def double_t():
+            nc.vector.tensor_scalar(out=t2[:], in0=t_raw[:], scalar1=2.0, scalar2=None, op0=ALU.mult)
 
-        s_extra = {
-            1: [lambda: cast_q(S, 3)],
-            2: [lambda: cast_k(S, 1, 0, 0, 32)],
-            3: [lambda: cast_k(S, 1, 0, 32, 64)],
-            7: [lambda: cast_v(S, 0, 0), lambda: cast_v(S, 0, 1)],
-            8: [lambda: cast_v(S, 1, 0)],
-            9: [lambda: cast_v(S, 1, 1)],
-            12: [lambda: square(0)],
-            13: [lambda: square(1), lambda: square(2)],
-            14: [lambda: square(3)],
-        }
-        v_extra = {
-            0: [lambda: cast_q(V, 2)],
-            1: [lambda: quant_q(2), lambda: score_pair(4)],
-            2: [lambda: quant_q(3)],
-            3: [lambda: cast_k(V, 1, 1, 0, 32), lambda: score_pair(6)],
-            4: [lambda: cast_k(V, 1, 1, 32, 64)],
-            5: [lambda: quant_k(1, 0, PASS), lambda: score_pair(8)],
-            7: [lambda: score_pair(10)],
-            8: [lambda: quant_v(0)],
-            9: [lambda: quant_v(1), lambda: score_pair(12)],
-            11: [lambda: score_pair(14), lambda: mix(0), lambda: mix(1), lambda: mix(2)],
-            12: [lambda: mix(3)],
-            13: [lambda: mix(4)],
-            14: [lambda: mix(5)],
-        }
-        for u in range(UNITS):
-            cap(u)
-            for job in s_extra.get(u, []):
-                job()
-            weigh(u)
-            if u > 0:
-                quant_w(u - 1)
-            for job in v_extra.get(u, []):
-                job()
+        nc.gpsimd.memset(warm[:], 0.0)
+        load(nc.scalar, t_raw[:], t_hbm)
+        nc.scalar.activation(out=warm_out[:], in_=warm[:], func=ACT.Tanh)
+        load(nc.sync, q_raw0[:], q_hbm[:, :, 0:QT])
+        for c in range(2):
+            load(nc.sync, k_raw[0][c][:], k_hbm[:, :, HALF * c:HALF * (c + 1)])
+        load(nc.sync, q_raw1[:], q_hbm[:, :, QT:2 * QT])
+        load(nc.sync, q_raw23[:], q_hbm[:, :, 2 * QT:])
+        for c in range(2):
+            load(nc.sync, k_raw[1][c][:], k_hbm[:, :, PASS + HALF * c:PASS + HALF * (c + 1)])
+        for g in range(PASSES):
+            load(nc.sync, v_raw[g][:], v_hbm[g])
+        load(nc.sync, gain[:], gn)
+        cast_q(V, 0, 128)
+        double_t()
+        quant_q(0, 128)
+        cast_k(S, 0, 0, 44, 64)
+        cast_k(V, 0, 0, 0, 44)
+        quant_k(0, 0, 64)
+        quant_k(0, 128, 64)
+        quant_k(0, 256, 64)
+        quant_k(0, 384, 64)
+        cast_k(S, 0, 1, 44, 64)
+        cast_k(V, 0, 1, 0, 44)
+        cast_q(S, 128, 256)
+        quant_k(0, 64, 64)
+        quant_k(0, 192, 64)
+        quant_k(0, 320, 64)
+        quant_k(0, 448, 64)
+        quant_q(128, 256)
+        score_pair(0)
+        cast_q(V, 256, 512)
+        cap(0)
+        score_pair(2)
+        cap(1)
+        weigh(0, 1)
+        cap(2)
+        quant_q(256, 512)
+        cast_k(V, 1, 0, 32, 64)
+        cap(3)
+        score_pair(4)
+        weigh(1, 2)
+        score_pair(6)
+        cast_k(V, 1, 1, 0, 64)
+        cap(4)
+        weigh(2, 4)
+        cast_k(S, 1, 0, 0, 32)
+        cap(5)
+        quant_k(1, 0, 512)
+        cap(6)
+        weigh(4, 6)
+        cap(7)
+        score_pair(8)
+        cast_v(S, 0, 0)
+        score_pair(10)
+        weigh(6, 8)
+        cast_v(S, 0, 1)
+        cap(8)
+        cast_v(V, 1, 1)
+        cap(9)
+        quant_w(0, 8)
+        score(12)
+        cast_v(S, 1, 0)
+        score(13)
+        cap(10)
+        weigh(8, 10)
+        cap(11)
+        score(14)
+        cap(12)
+        quant_v(0, 4)
+        score(15)
+        cap(13)
+        quant_w(8, 10)
+        weigh(10, 12)
+        cap(14)
+        mix(0)
+        mix(1)
+        cap(15)
+        weigh(12, 14)
+        square(0)
+        square(1)
+        quant_w(10, 12)
+        weigh(14, 15)
+        mix(2)
+        mix(3)
+        quant_w(12, 14)
+        norm(0, 2)
+        weigh(15, 16)
+        square(2)
+        mix(4)
+        square(3)
+        mix(5)
+        quant_w(14, 15)
+        quant_w(15, 16)
+        norm(2, 4)
         mix(6)
-        quant_w(UNITS - 1)
-        mix(7)
+        finish(0)
         square(4)
-        norm(0, 5)
+        finish(1)
+        mix(7)
         square(5)
+        finish(2)
+        store(0, 0, 2)
+        finish(3)
+        norm(4, 6)
         square(6)
-        norm(5, 7)
+        store(1, 0, 2)
+        finish(4)
         square(7)
-        norm(7, 8)
-        for o in range(QTILES * H):
-            finish(o)
-            if o in (1, 3, 5):
-                store(o // H, 0, H)
-            elif o >= 6:
-                store(o // H, o % H, o % H + 1)
+        finish(5)
+        norm(6, 8)
+        store(2, 0, 2)
+        finish(6)
+        finish(7)
+        store(3, 0, 2)

@@ -71,7 +71,7 @@ def tile_rows_a_relu_cap_onorm_kernel(tc, qT, kT, t, v, gn, out):
 
         s_bank = [[ps.tile([P, PACK * QT], F32, name=f"s_bank{h}{b}") for b in range(2)] for h in range(H)]
         y_bank = [ps.tile([P, 4 * E], F32, name=f"y_bank{b}") for b in range(4)]
-        y_place = [(0, 0), (0, 1), (1, 0), (1, 1), (2, 0), (2, 1), (3, 0), (3, 1)]
+        y_place = [(0, 0), (0, 1), (1, 0), (1, 1), (0, 2), (0, 3), (2, 0), (3, 0)]
 
         def y_ap(o):
             b, c = y_place[o]
@@ -93,9 +93,9 @@ def tile_rows_a_relu_cap_onorm_kernel(tc, qT, kT, t, v, gn, out):
         def cast_v(eng, g, h):
             interleave(eng, v_bf[:, H * g + h, :], v_raw[g][:, h, :].rearrange("p (j e) -> p j e", j=PACK))
 
-        def cast_k(eng, g, c, s0, s1):
-            dst = k_bf[g][:, :, 64 * c + s0:64 * c + s1, :].rearrange("p r s j -> p s j r")
-            src = k_raw[g][c][:, :, PACK * s0:PACK * s1].rearrange("p j (s r) -> p s j r", r=PACK)
+        def cast_k(eng, g, c, s0, s1, r0=0, r1=PACK):
+            dst = k_bf[g][:, r0:r1, 64 * c + s0:64 * c + s1, :].rearrange("p r s j -> p s j r")
+            src = k_raw[g][c][:, :, PACK * s0:PACK * s1].rearrange("p j (s r) -> p s j r", r=PACK)[:, :, :, r0:r1]
             copy(eng, dst, src)
 
         def quant(codes, scales, src):
@@ -158,9 +158,9 @@ def tile_rows_a_relu_cap_onorm_kernel(tc, qT, kT, t, v, gn, out):
                 op1=ALU.mult,
             )
 
-        def mix(o):
+        def mix(o, passes=range(PASSES)):
             h = o % H
-            for g in range(PASSES):
+            for g in passes:
                 u = g * QTILES * H + o
                 cols = slice(E * (H * g + h), E * (H * g + h + 1))
                 nc.tensor.matmul_mx(
@@ -172,6 +172,12 @@ def tile_rows_a_relu_cap_onorm_kernel(tc, qT, kT, t, v, gn, out):
                     start=(g == 0),
                     stop=(g == PASSES - 1),
                 )
+
+        def mix_open(o):
+            mix(o, [0])
+
+        def mix_close(o):
+            mix(o, [1])
 
         def square(o):
             nc.scalar.activation(out=squares[:, o, :], in_=y_ap(o), func=ACT.Square, scale=1.0 / 16.0, accum_out=sumsq[:, o:o + 1])
@@ -216,8 +222,10 @@ def tile_rows_a_relu_cap_onorm_kernel(tc, qT, kT, t, v, gn, out):
         quant_k(0, 128, 64)
         quant_k(0, 256, 64)
         quant_k(0, 384, 64)
-        cast_k(S, 0, 1, 44, 64)
-        cast_k(V, 0, 1, 0, 44)
+        cast_k(S, 0, 1, 44, 64, 0, 2)
+        cast_k(V, 0, 1, 0, 44, 0, 2)
+        cast_k(S, 0, 1, 44, 64, 2, 4)
+        cast_k(V, 0, 1, 0, 44, 2, 4)
         cast_q(S, 128, 256)
         quant_k(0, 64, 64)
         quant_k(0, 192, 64)
@@ -232,80 +240,84 @@ def tile_rows_a_relu_cap_onorm_kernel(tc, qT, kT, t, v, gn, out):
         weigh(0, 1)
         cap(2)
         quant_q(256, 512)
+        weigh(1, 2)
+        cast_k(S, 1, 0, 0, 32)
+        score_pair(4)
         cast_k(V, 1, 0, 32, 64)
         cap(3)
-        score_pair(4)
-        weigh(1, 2)
+        cast_k(V, 1, 1, 32, 64)
+        cast_k(S, 1, 1, 0, 32)
         score_pair(6)
-        cast_k(V, 1, 1, 0, 64)
-        cap(4)
         weigh(2, 4)
-        cast_k(S, 1, 0, 0, 32)
+        cap(4)
         cap(5)
         quant_k(1, 0, 512)
         cap(6)
         weigh(4, 6)
-        cap(7)
         score_pair(8)
+        cap(7)
         cast_v(S, 0, 0)
         score_pair(10)
         weigh(6, 8)
-        cast_v(S, 0, 1)
         cap(8)
-        cast_v(V, 1, 1)
         cap(9)
-        quant_w(0, 8)
+        cast_v(V, 0, 1)
         score(12)
-        cast_v(S, 1, 0)
-        score(13)
+        quant_w(0, 8)
         cap(10)
-        weigh(8, 10)
-        cap(11)
+        score(13)
+        cast_v(S, 1, 0)
         score(14)
-        cap(12)
+        weigh(8, 10)
+        cast_v(S, 1, 1)
+        cap(11)
         quant_v(0, 4)
+        cap(12)
         score(15)
-        cap(13)
         quant_w(8, 10)
+        cap(13)
         weigh(10, 12)
-        cap(14)
         mix(0)
+        cap(14)
         mix(1)
+        mix_open(7)
         cap(15)
         weigh(12, 14)
         square(0)
         square(1)
         quant_w(10, 12)
-        weigh(14, 15)
-        mix(2)
-        mix(3)
         quant_w(12, 14)
-        norm(0, 2)
-        weigh(15, 16)
-        square(2)
+        mix(2)
+        weigh(14, 15)
+        mix(3)
         mix(4)
-        square(3)
+        weigh(15, 16)
+        norm(0, 2)
         mix(5)
+        square(2)
+        square(3)
         quant_w(14, 15)
+        square(4)
         quant_w(15, 16)
         norm(2, 4)
-        mix(6)
-        finish(0)
-        square(4)
-        finish(1)
-        mix(7)
         square(5)
+        mix(6)
         finish(2)
-        store(0, 0, 2)
+        mix_close(7)
         finish(3)
-        norm(4, 6)
         square(6)
+        finish(0)
         store(1, 0, 2)
-        finish(4)
+        finish(1)
+        norm(4, 6)
         square(7)
+        finish(4)
+        store(0, 0, 2)
+        norm(6, 7)
         finish(5)
-        norm(6, 8)
-        store(2, 0, 2)
+        norm(7, 8)
         finish(6)
+        store(2, 0, 2)
         finish(7)
-        store(3, 0, 2)
+        store(3, 0, 1)
+        store(3, 1, 2)

@@ -66,12 +66,10 @@ def tile_rows_a_relu_cap_onorm_kernel(tc, qT, kT, t, v, gn, out):
         sumsq = tile("sumsq", [P, QTILES * H], F32)
         rstd = tile("rstd", [P, QTILES * H], F32)
         result = [tile(f"result{i}", [P, H, E], F32) for i in range(QTILES)]
-        warm = tile("warm", [P, 1], F32)
-        warm_out = tile("warm_out", [P, 1], F32)
 
         s_bank = [[ps.tile([P, PACK * QT], F32, name=f"s_bank{h}{b}") for b in range(2)] for h in range(H)]
         y_bank = [ps.tile([P, 4 * E], F32, name=f"y_bank{b}") for b in range(4)]
-        y_place = [(0, 0), (0, 1), (1, 0), (1, 1), (0, 2), (0, 3), (2, 0), (3, 0)]
+        y_place = [(0, 0), (0, 1), (1, 0), (1, 1), (2, 0), (2, 1), (3, 0), (3, 1)]
 
         def y_ap(o):
             b, c = y_place[o]
@@ -94,8 +92,8 @@ def tile_rows_a_relu_cap_onorm_kernel(tc, qT, kT, t, v, gn, out):
             interleave(eng, v_bf[:, H * g + h, :], v_raw[g][:, h, :].rearrange("p (j e) -> p j e", j=PACK))
 
         def cast_k(eng, g, c, s0, s1, r0=0, r1=PACK):
-            dst = k_bf[g][:, r0:r1, 64 * c + s0:64 * c + s1, :].rearrange("p r s j -> p s j r")
-            src = k_raw[g][c][:, :, PACK * s0:PACK * s1].rearrange("p j (s r) -> p s j r", r=PACK)[:, :, :, r0:r1]
+            dst = k_bf[g][:, r0:r1, 64 * c + s0:64 * c + s1, :].rearrange("p r (a b) j -> p a j b r", b=2)
+            src = k_raw[g][c][:, :, PACK * s0:PACK * s1].rearrange("p j (a b r) -> p a j b r", b=2, r=PACK)[:, :, :, :, r0:r1]
             copy(eng, dst, src)
 
         def quant(codes, scales, src):
@@ -198,11 +196,9 @@ def tile_rows_a_relu_cap_onorm_kernel(tc, qT, kT, t, v, gn, out):
 
         S, V = nc.scalar, nc.vector
         def double_t():
-            nc.vector.tensor_scalar(out=t2[:], in0=t_raw[:], scalar1=2.0, scalar2=None, op0=ALU.mult)
+            nc.scalar.activation(out=t2[:], in_=t_raw[:], func=ACT.Copy, scale=2.0)
 
-        nc.gpsimd.memset(warm[:], 0.0)
         load(nc.scalar, t_raw[:], t_hbm)
-        nc.scalar.activation(out=warm_out[:], in_=warm[:], func=ACT.Tanh)
         load(nc.sync, q_raw0[:], q_hbm[:, :, 0:QT])
         for c in range(2):
             load(nc.sync, k_raw[0][c][:], k_hbm[:, :, HALF * c:HALF * (c + 1)])
@@ -213,8 +209,8 @@ def tile_rows_a_relu_cap_onorm_kernel(tc, qT, kT, t, v, gn, out):
         for g in range(PASSES):
             load(nc.sync, v_raw[g][:], v_hbm[g])
         load(nc.sync, gain[:], gn)
-        cast_q(V, 0, 128)
         double_t()
+        cast_q(V, 0, 128)
         quant_q(0, 128)
         cast_k(S, 0, 0, 44, 64)
         cast_k(V, 0, 0, 0, 44)
@@ -240,47 +236,43 @@ def tile_rows_a_relu_cap_onorm_kernel(tc, qT, kT, t, v, gn, out):
         weigh(0, 1)
         cap(2)
         quant_q(256, 512)
-        weigh(1, 2)
-        cast_k(S, 1, 0, 0, 32)
-        score_pair(4)
-        cast_k(V, 1, 0, 32, 64)
+        cast_k(V, 1, 0, 0, 64)
         cap(3)
+        score_pair(4)
         cast_k(V, 1, 1, 32, 64)
         cast_k(S, 1, 1, 0, 32)
         score_pair(6)
-        weigh(2, 4)
+        weigh(1, 2)
         cap(4)
-        cap(5)
         quant_k(1, 0, 512)
+        cap(5)
+        weigh(2, 4)
         cap(6)
-        weigh(4, 6)
         score_pair(8)
         cap(7)
-        cast_v(S, 0, 0)
-        score_pair(10)
-        weigh(6, 8)
+        weigh(4, 6)
         cap(8)
+        score_pair(10)
         cap(9)
-        cast_v(V, 0, 1)
-        score(12)
+        weigh(6, 8)
+        cast_v(S, 0, 0)
+        score_pair(12)
+        cast_v(S, 0, 1)
+        weigh(8, 10)
+        cast_v(S, 1, 0)
+        cast_v(S, 1, 1)
         quant_w(0, 8)
         cap(10)
-        score(13)
-        cast_v(S, 1, 0)
-        score(14)
-        weigh(8, 10)
-        cast_v(S, 1, 1)
         cap(11)
-        quant_v(0, 4)
-        cap(12)
-        score(15)
         quant_w(8, 10)
+        cap(12)
+        quant_v(0, 4)
+        score_pair(14)
         cap(13)
         weigh(10, 12)
         mix(0)
-        cap(14)
         mix(1)
-        mix_open(7)
+        cap(14)
         cap(15)
         weigh(12, 14)
         square(0)
@@ -292,32 +284,32 @@ def tile_rows_a_relu_cap_onorm_kernel(tc, qT, kT, t, v, gn, out):
         mix(3)
         mix(4)
         weigh(15, 16)
-        norm(0, 2)
         mix(5)
+        norm(0, 2)
         square(2)
-        square(3)
         quant_w(14, 15)
-        square(4)
+        square(3)
         quant_w(15, 16)
-        norm(2, 4)
-        square(5)
+        square(4)
         mix(6)
-        finish(2)
-        mix_close(7)
-        finish(3)
-        square(6)
         finish(0)
-        store(1, 0, 2)
+        square(5)
         finish(1)
+        mix(7)
+        norm(2, 4)
         norm(4, 6)
-        square(7)
-        finish(4)
         store(0, 0, 2)
-        norm(6, 7)
+        finish(2)
+        square(6)
+        finish(3)
+        finish(4)
+        square(7)
+        store(1, 0, 2)
         finish(5)
+        norm(6, 7)
         norm(7, 8)
-        finish(6)
         store(2, 0, 2)
+        finish(6)
         finish(7)
         store(3, 0, 1)
         store(3, 1, 2)

from contextlib import ExitStack

import concourse.mybir as mybir

H, D, NQ, N, E = 2, 256, 512, 1024, 128
FLOPS = 2 * H * N * NQ * (D + E)

F32 = mybir.dt.float32
BF16 = mybir.dt.bfloat16
U32 = mybir.dt.uint32
U8 = mybir.dt.uint8
FP8X4 = mybir.dt.float8_e4m3fn_x4
ACT = mybir.ActivationFunctionType
ALU = mybir.AluOpType

P = 128
PACK = 4
ROWS = D // PACK
PASS = P * PACK
PASSES = N // PASS
QT = 128
QTILES = NQ // QT
UNITS = PASSES * QTILES * H
HALF = PASS // 2


def tile_rows_a_relu_cap_onorm_kernel(tc, qT, kT, t, v, gn, out):
    nc = tc.nc
    with ExitStack() as ctx:
        sb = ctx.enter_context(tc.tile_pool(name="sb", bufs=1))
        ps = ctx.enter_context(tc.psum_pool(name="ps", bufs=1))
        ctx.enter_context(tc.manual_schedule())

        def tile(name, shape, dtype):
            return sb.tile(shape, dtype, name=name, align_bytes=64)

        q_hbm = qT.rearrange("h (p j) q -> (h p) j q", j=PACK)
        k_hbm = kT.rearrange("h (p j) n -> (h p) j n", j=PACK)
        v_hbm = v.rearrange("h (g p j) e -> g p h (j e)", g=PASSES, j=PACK)
        t_hbm = t.rearrange("(g p j) o -> p g (j o)", g=PASSES, j=PACK)

        q_raw0 = tile("q_raw0", [P, PACK, QT], F32)
        q_raw1 = tile("q_raw1", [P, PACK, QT], F32)
        q_raw23 = tile("q_raw23", [P, PACK, 2 * QT], F32)
        q_raw = {0: q_raw0, 1: q_raw1, 2: q_raw23, 3: q_raw23}
        k_raw = [[tile(f"k_raw{g}{c}", [P, PACK, HALF], F32) for c in range(2)] for g in range(PASSES)]
        v_raw = [tile(f"v_raw{g}", [P, H, PACK * E], F32) for g in range(PASSES)]
        t_raw = tile("t_raw", [P, PASSES, PACK], F32)
        t2 = tile("t2", [P, PASSES, PACK], F32)
        gain = tile("gain", [P, E], F32)

        q_bf = tile("q_bf", [P, NQ * PACK], BF16)
        q_codes = tile("q_codes", [P, NQ], U32)
        q_scales = tile("q_scales", [P, NQ], U8)
        k_bf = [tile(f"k_bf{g}", [P, PACK, P, PACK], BF16) for g in range(PASSES)]
        k_codes = [tile(f"k_codes{g}", [P, PASS], U32) for g in range(PASSES)]
        k_scales = [tile(f"k_scales{g}", [P, PASS], U8) for g in range(PASSES)]
        v_bf = tile("v_bf", [P, PASSES * H, E * PACK], BF16)
        v_codes = tile("v_codes", [P, PASSES * H * E], U32)
        v_scales = tile("v_scales", [P, PASSES * H * E], U8)
        capped = tile("capped", [P, UNITS * QT, PACK], F32)
        w_bf = tile("w_bf", [P, UNITS * QT, PACK], BF16)
        w_codes = tile("w_codes", [P, UNITS * QT], U32)
        w_scales = tile("w_scales", [P, UNITS * QT], U8)
        squares = tile("squares", [P, QTILES * H, E], BF16)
        sumsq = tile("sumsq", [P, QTILES * H], F32)
        rstd = tile("rstd", [P, QTILES * H], F32)
        result = [tile(f"result{i}", [P, H, E], F32) for i in range(QTILES)]

        s_bank = [[ps.tile([P, PACK * QT], F32, name=f"s_bank{h}{b}") for b in range(2)] for h in range(H)]
        y_bank = [ps.tile([P, 4 * E], F32, name=f"y_bank{b}") for b in range(4)]
        y_place = [(0, 0), (0, 1), (1, 0), (1, 1), (2, 0), (2, 1), (3, 0), (3, 1)]

        def y_ap(o):
            b, c = y_place[o]
            return y_bank[b][:, c * E:(c + 1) * E]

        def copy(eng, dst, src):
            if eng is nc.scalar:
                nc.scalar.copy(out=dst, in_=src)
            else:
                nc.vector.tensor_copy(out=dst, in_=src)

        def interleave(eng, dst, src):
            copy(eng, dst.rearrange("p (c i j) -> p c j i", i=4, j=PACK), src.rearrange("p j (c i) -> p c j i", i=4))

        def cast_q(eng, q0, q1):
            first = min(q0 // QT, 2) * QT
            interleave(eng, q_bf[:, PACK * q0:PACK * q1], q_raw[q0 // QT][:, :, q0 - first:q1 - first])

        def cast_v(eng, g, h):
            interleave(eng, v_bf[:, H * g + h, :], v_raw[g][:, h, :].rearrange("p (j e) -> p j e", j=PACK))

        def cast_k(eng, g, c, s0, s1, r0=0, r1=PACK):
            dst = k_bf[g][:, r0:r1, 64 * c + s0:64 * c + s1, :].rearrange("p r (a b) j -> p a j b r", b=2)
            src = k_raw[g][c][:, :, PACK * s0:PACK * s1].rearrange("p j (a b r) -> p a j b r", b=2, r=PACK)[:, :, :, :, r0:r1]
            copy(eng, dst, src)

        def quant(codes, scales, src):
            nc.vector.quantize_mx(out=codes.bitcast(FP8X4), scales=scales, in_=src)

        def quant_q(q0, q1):
            quant(q_codes[:, q0:q1], q_scales[:, q0:q1], q_bf[:, PACK * q0:PACK * q1])

        def quant_k(g, col0, cols):
            flat = k_bf[g][:].rearrange("p r s j -> p (r s j)")
            quant(k_codes[g][:, col0:col0 + cols], k_scales[g][:, col0:col0 + cols], flat[:, PACK * col0:PACK * (col0 + cols)])

        def quant_v(a, b):
            quant(v_codes[:, E * a:E * b], v_scales[:, E * a:E * b], v_bf[:, a:b, :].rearrange("p h x -> p (h x)"))

        def quant_w(a, b):
            cols = slice(QT * a, QT * b)
            quant(w_codes[:, cols], w_scales[:, cols], w_bf[:, cols, :].rearrange("p q r -> p (q r)"))

        def unit(u):
            return u // (QTILES * H), (u // H) % QTILES, u % H

        def score_r(u, r):
            g, i, h = unit(u)
            rows = slice(ROWS * h, ROWS * (h + 1))
            cols = slice(P * r, P * (r + 1))
            nc.tensor.matmul_mx(
                out=s_bank[h][(u // H) % 2][:, QT * r:QT * (r + 1)],
                lhsT=k_codes[g][rows, cols].bitcast(FP8X4),
                lhsT_scale=k_scales[g][rows, cols],
                rhs=q_codes[rows, QT * i:QT * (i + 1)].bitcast(FP8X4),
                rhs_scale=q_scales[rows, QT * i:QT * (i + 1)],
                start=True,
                stop=True,
            )

        def score(u):
            for r in range(PACK):
                score_r(u, r)

        def score_pair(u):
            for r in range(PACK):
                score_r(u, r)
                score_r(u + 1, r)

        def cap(u):
            g, i, h = unit(u)
            src = s_bank[h][(u // H) % 2][:].rearrange("p (r q) -> p q r", r=PACK)
            nc.scalar.activation(out=capped[:, QT * u:QT * (u + 1), :], in_=src, func=ACT.Tanh, scale=0.5)

        def weigh(a, b):
            g = a // (QTILES * H)
            cols = slice(QT * a, QT * b)
            nc.vector.scalar_tensor_tensor(
                out=w_bf[:, cols, :],
                in0=capped[:, cols, :],
                scalar=0.0,
                in1=t2[:, g:g + 1, :].broadcast_to([P, QT * (b - a), PACK]),
                op0=ALU.max,
                op1=ALU.mult,
            )

        def mix(o, passes=range(PASSES)):
            h = o % H
            for g in passes:
                u = g * QTILES * H + o
                cols = slice(E * (H * g + h), E * (H * g + h + 1))
                nc.tensor.matmul_mx(
                    out=y_ap(o),
                    lhsT=w_codes[:, QT * u:QT * (u + 1)].bitcast(FP8X4),
                    lhsT_scale=w_scales[:, QT * u:QT * (u + 1)],
                    rhs=v_codes[:, cols].bitcast(FP8X4),
                    rhs_scale=v_scales[:, cols],
                    start=(g == 0),
                    stop=(g == PASSES - 1),
                )

        def mix_open(o):
            mix(o, [0])

        def mix_close(o):
            mix(o, [1])

        def square(o):
            nc.scalar.activation(out=squares[:, o, :], in_=y_ap(o), func=ACT.Square, scale=1.0 / 16.0, accum_out=sumsq[:, o:o + 1])

        def norm(o0, o1):
            nc.scalar.activation(out=rstd[:, o0:o1], in_=sumsq[:, o0:o1], func=ACT.Abs_reciprocal_sqrt, scale=256.0 / E, bias=256.0 * 1e-5)

        def finish(o):
            nc.vector.scalar_tensor_tensor(
                out=result[o // H][:, o % H, :], in0=y_ap(o), scalar=rstd[:, o:o + 1], in1=gain[:], op0=ALU.mult, op1=ALU.mult
            )

        def store(i, h0, h1):
            nc.sync.dma_start(out=out[h0:h1, QT * i:QT * (i + 1), :].rearrange("h q e -> q h e"), in_=result[i][:, h0:h1, :])

        def load(eng, dst, src):
            eng.dma_start(out=dst, in_=src)

        S, V = nc.scalar, nc.vector
        def double_t():
            nc.scalar.activation(out=t2[:], in_=t_raw[:], func=ACT.Copy, scale=2.0)

        load(nc.scalar, t_raw[:], t_hbm)
        load(nc.sync, q_raw0[:], q_hbm[:, :, 0:QT])
        for c in range(2):
            load(nc.sync, k_raw[0][c][:], k_hbm[:, :, HALF * c:HALF * (c + 1)])
        load(nc.sync, q_raw1[:], q_hbm[:, :, QT:2 * QT])
        load(nc.sync, q_raw23[:], q_hbm[:, :, 2 * QT:])
        for c in range(2):
            load(nc.sync, k_raw[1][c][:], k_hbm[:, :, PASS + HALF * c:PASS + HALF * (c + 1)])
        for g in range(PASSES):
            load(nc.sync, v_raw[g][:], v_hbm[g])
        load(nc.sync, gain[:], gn)
        double_t()
        cast_q(V, 0, 128)
        quant_q(0, 128)
        cast_k(S, 0, 0, 44, 64)
        cast_k(V, 0, 0, 0, 44)
        quant_k(0, 0, 64)
        quant_k(0, 128, 64)
        quant_k(0, 256, 64)
        quant_k(0, 384, 64)
        cast_k(S, 0, 1, 44, 64, 0, 2)
        cast_k(V, 0, 1, 0, 44, 0, 2)
        cast_k(S, 0, 1, 44, 64, 2, 4)
        cast_k(V, 0, 1, 0, 44, 2, 4)
        cast_q(S, 128, 256)
        quant_k(0, 64, 64)
        quant_k(0, 192, 64)
        quant_k(0, 320, 64)
        quant_k(0, 448, 64)
        quant_q(128, 256)
        score_pair(0)
        cast_q(V, 256, 512)
        cap(0)
        score_pair(2)
        cap(1)
        weigh(0, 1)
        cap(2)
        quant_q(256, 512)
        cast_k(V, 1, 0, 0, 64)
        cap(3)
        score_pair(4)
        cast_k(V, 1, 1, 32, 64)
        cast_k(S, 1, 1, 0, 32)
        score_pair(6)
        weigh(1, 2)
        cap(4)
        quant_k(1, 0, 512)
        cap(5)
        weigh(2, 4)
        cap(6)
        score_pair(8)
        cap(7)
        weigh(4, 6)
        cap(8)
        score_pair(10)
        cap(9)
        weigh(6, 8)
        cast_v(S, 0, 0)
        score_pair(12)
        cast_v(S, 0, 1)
        weigh(8, 10)
        cast_v(S, 1, 0)
        cast_v(S, 1, 1)
        quant_w(0, 8)
        cap(10)
        cap(11)
        quant_w(8, 10)
        cap(12)
        quant_v(0, 4)
        score_pair(14)
        cap(13)
        weigh(10, 12)
        mix(0)
        mix(1)
        cap(14)
        cap(15)
        weigh(12, 14)
        square(0)
        square(1)
        quant_w(10, 12)
        quant_w(12, 14)
        mix(2)
        weigh(14, 15)
        mix(3)
        mix(4)
        weigh(15, 16)
        mix(5)
        norm(0, 2)
        square(2)
        quant_w(14, 15)
        square(3)
        quant_w(15, 16)
        square(4)
        mix(6)
        finish(0)
        square(5)
        finish(1)
        mix(7)
        norm(2, 4)
        norm(4, 6)
        store(0, 0, 2)
        finish(2)
        square(6)
        finish(3)
        finish(4)
        square(7)
        store(1, 0, 2)
        finish(5)
        norm(6, 7)
        norm(7, 8)
        store(2, 0, 2)
        finish(6)
        finish(7)
        store(3, 0, 1)
        store(3, 1, 2)
